import numpy as np, ml_dtypes
CORES = [25,29,65,69,153,157,193,197]
N = 8
import mx_ref
BF = ml_dtypes.bfloat16
def gentries(a):
    return np.ascontiguousarray(a.reshape(8, 16, -1).transpose(0, 2, 1)).reshape(8, -1)
def gtable(e):
    e = np.asarray(e); return np.ascontiguousarray(e.reshape(8, -1, 16).transpose(0, 2, 1)).reshape(128, -1).astype(np.int32)
def gcols(t, e):
    v = np.concatenate([t.reshape(8, 16, -1, 4), np.zeros((8, 16, 1, 4), BF)], axis=2)
    return np.ascontiguousarray(np.stack([v[g][:, e[g]] for g in range(8)])).reshape(128, -1)
def gpick(z, e):
    return np.concatenate([z[16 * g:16 * g + 16][:, e[g]] for g in range(8)])
def tile(rs):
    return np.stack(rs, axis=2).reshape(128, -1).astype(BF)
def pick(q, e):
    c = np.concatenate([q[0].reshape(128, -1, 4), np.zeros((128, 1, 4), np.uint8)], axis=1); s = np.concatenate([q[1], np.ones((16, 1), np.uint8)], axis=1)
    return (np.ascontiguousarray(c[:, e].reshape(128, -1)), np.ascontiguousarray(s[:, e]))
def join(*qs):
    return (np.concatenate([q[0] for q in qs], axis=1), np.concatenate([q[1] for q in qs], axis=1))
def put(q, e, v):
    c, s = q[0].reshape(128, -1, 4).copy(), q[1].copy(); c[:, e] = v[0].reshape(128, -1, 4); s[:, e] = v[1]
    return (c.reshape(128, -1), s)
def pk(c, s):
    return (np.ascontiguousarray(c), mx_ref.live(s))
def emit(q):
    return q[0], q[1]
def packed(v, rng):
    q = [mx_ref.quantize(np.ascontiguousarray(v[r])) for r in range(N)]
    return np.stack([a for a, b in q]), np.stack([mx_ref.plane(b, rng) for a, b in q])
def values_of_codes():
    e, c = np.zeros((128, 128, 4), np.float32), np.zeros((128, 2, 4), np.uint8)
    e[np.arange(128), np.arange(128), 0] = 1
    c[:127, :, 0] = np.arange(256).reshape(2, 128).T[:127]
    return mx_ref.matmul(mx_ref.quantize(e.reshape(128, 512).astype(BF)), (c.reshape(128, 8), np.full((16, 2), 127, np.uint8))).T.reshape(-1).astype(np.float64)
CODE_VALUE, SCALE_VALUE = values_of_codes(), 2.0 ** (np.arange(256) - 127.0)
def decode(q):
    return (CODE_VALUE[q[0]].reshape(16, 8, -1, 4) * SCALE_VALUE[q[1]][:, None, :, None] + 0.0).reshape(128, -1).astype(np.float32)
def f(rng, *shape):
    return mx_ref.flush((rng.standard_normal(shape, dtype=np.float32) * np.exp2(rng.integers(-2, 3, shape[:-1] + (1,)))).astype(BF))
def wide(rng, *shape, cols=0):
    v = rng.standard_normal(shape, dtype=np.float32) * np.exp2(rng.integers(-12, 13, shape)).astype(np.float32)
    if cols: v *= np.repeat(np.exp2(rng.integers(-cols, cols + 1, shape[:-2] + (1, shape[-1] // 4))) * (rng.random(shape[:-2] + (1, shape[-1] // 4)) > 0.0625), 4, axis=-1).astype(np.float32)
    return mx_ref.flush(v.astype(BF))
C, E, B, K, R = 400, 20, 4, 80, 3
STEP = [1, 2, 4]
LO, HI = 2, 6
def gaps(p):
    return np.argmin(p[::16].reshape(8, E, E) + np.float32(0.0), axis=2)
def starts(a, c):
    s, free = np.full(a.shape, -1), np.zeros(c.shape, int)
    for k in range(B):
        n = a[:, :, k]
        i = np.where((c >= free) & (c < free + n), c + 1, free)
        fits = i + n <= E
        s[:, :, k] = np.where(fits, i, -1)
        free = np.where(fits, i + n + 1, free)
    return s
def solve(a, c):
    left = starts(a, c)
    m = starts(a[:, :, ::-1], E - 1 - c)[:, :, ::-1]
    end = E - 1 - m
    first, last = np.maximum(left, end - a + 1), np.minimum(left + a - 1, end)
    sure = (left >= 0) & (m >= 0) & (first <= last)
    line = E * np.arange(E)[None, :, None]
    return np.where(sure, line + left, -1).reshape(8, K), np.where(sure, line + end, -1).reshape(8, K), np.where(sure, first, -1), np.where(sure, last, -1)
def fallen(first, last):
    cell = np.arange(E)
    inside = (cell >= first[:, :, :, None]) & (cell <= last[:, :, :, None])
    e = np.where(inside.any(axis=2), B * cell[None, :, None] + np.argmax(inside, axis=2), -1)
    return np.ascontiguousarray(e.transpose(0, 2, 1)).reshape(8, C)
def numbers_of(rng):
    return {"x": np.array(f(rng, N, 128, 4 * C)), "u": np.array(f(rng, N, 128, 512)), "v": np.array(f(rng, N, 128, 512))}
def weights(rng, still=[]):
    w = np.array(f(rng, N, 128, 2048)).reshape(N, 8, 16, 4, 8, 16, 4)
    for i in still:
        w[:, :, i] = 0
        w[:, :, :, :, :, i] = 0
    c, p = packed(w.reshape(N, 128, 2048), rng)
    return {"wc": c, "ws": p}
def lengths(rng):
    return rng.integers(LO, HI + 1, (N, 8, E, B))
def blocks(a):
    return {"bl": np.stack([gtable(a[r].reshape(8, K)) for r in range(N)])}
def signs(rng):
    return np.stack([rng.permutation(8) % 2 * 2.0 - 1.0 for r in range(N)])
def setup_inputs(rng):
    return {**numbers_of(rng), **weights(rng), **blocks(lengths(rng))}
def setup_inputs_ties(rng):
    d = numbers_of(rng)
    e = rng.permutation(N)
    x = d["x"].reshape(N, 8, 16, C, 4)
    for r in range(N):
        for g in range(8):
            k = np.zeros(C, int) if r == e[0] else rng.permutation(C) % 3
            a = x[r, g, :8, :3].copy()
            a[:, 2] = 0
            x[r, g, :8] = a[:, k]
    x[e[1]] = 0
    u = d["u"].reshape(N, 8, 16, 8, 16, 4)
    k = u.copy()
    u[:, :, :, :, 0] = 0
    for g in range(8): u[:, g, :8, g, 0] = k[:, g, :8, g, 0]
    return {"x": x.reshape(N, 128, 4 * C), "u": u.reshape(N, 128, 512), "v": d["v"], **weights(rng, range(8)), **blocks(lengths(rng))}
def setup_inputs_near(rng):
    d = numbers_of(rng)
    x = d["x"].astype(np.float32).reshape(N, 8, 16, C, 4)
    u = d["u"].reshape(N, 128, 128, 4)
    u[:, :, ::16] = 0
    x[:, :, 0] = 0
    o, c, far = rng.permutation(N) % 4, signs(rng), signs(rng)
    j = np.arange(E)
    for r in range(N):
        i = (j + rng.integers(0, E, (8, E, 1))) % E
        twos = rng.integers(0, 2, (8, E, 1)) > 0
        if o[r] == 3:
            i = i % (E // 2) * 2 + j // (E // 2)
            twos = twos | True
        s = (np.where(twos, (E - 1 - i) // 2, E - 1 - i) + rng.integers(1, 200, (8, E, 1))).reshape(8, C)
        i = i.reshape(8, C)
        size = 1.0 if o[r] < 2 else 2.0 ** -4
        g = ((s[:, :, None] >> np.arange(8)) & 1) * np.exp2(np.arange(8) - 23.0) * size
        x[r, :, 8:] = rng.integers(4, 8, (8, 8, C, 4)) * 2.0 ** -20 * size
        x[r, :, 8] = g[:, :, :4]
        x[r, :, 9] = g[:, :, 4:]
        if o[r] < 2: x[r, :, 0, :, 0] = np.where((i == 0) & (far[r][:, None] > 0), 2.0 ** 30, c[r][:, None])
        if o[r] == 3:
            x[r, :, 10] = 0
            x[r, :, 10, :, 0] = (9 - i % 2) * 2.0 ** -30
        k = 1.0 if o[r] == 0 else 2.0 ** -30
        for h in range(0, 128, 16):
            u[r, h, h, 0] = k
            u[r, h + 8:h + 10, h] = k
            if o[r] == 3: u[r, h + 10, h, 0] = k
    return {"x": x.reshape(N, 128, 4 * C).astype(BF), "u": u.reshape(N, 128, 512), "v": d["v"], **weights(rng, [0, 8, 9, 10, 11, 12, 13, 14, 15]), **blocks(lengths(rng))}
def setup_inputs_huge(rng):
    d = numbers_of(rng)
    c = np.stack([rng.permutation(C) % 2 * 2.0 - 1.0 for r in range(N)])
    c[rng.permutation(N) < N // 2] = 1
    x = 2.0 ** 30 * (0.55 + 0.15 * rng.random((N, 128, C, 4))) * c[:, None, :, None]
    u = d["u"].reshape(N, 128, 128, 4)
    a = 2.0 ** 30 * (1 - 0.25 * rng.random((N, 128, 8, 4))) * signs(rng)[:, None, :, None]
    u[:, :, ::16] = a.astype(np.float32).astype(BF)
    w = np.zeros((N, 128, 4, 128, 4), np.float32)
    i = np.arange(128)
    for b in range(4): w[:, i, b, i, b] = -1
    wc, ws = packed(w.reshape(N, 128, 2048).astype(BF), rng)
    return {"x": x.astype(np.float32).reshape(N, 128, 4 * C).astype(BF), "u": u.reshape(N, 128, 512), "v": d["v"], "wc": wc, "ws": ws, **blocks(lengths(rng))}
def setup_inputs_packs(rng):
    d = numbers_of(rng)
    x = d["x"].reshape(N, 8, 16, C, 4)
    u = d["u"].reshape(N, 128, 128, 4)
    a = lengths(rng)
    gap = np.where(rng.random((N, 8, E)) < 0.25, rng.integers(0, 2, (N, 8, E)) * (E - 1), rng.integers(0, E, (N, 8, E)))
    ends = np.sort(np.argsort(rng.random((N, 8, E, E - B)), axis=3)[:, :, :, :B - 1], axis=3) + 1
    full = np.diff(ends, axis=3, prepend=0, append=E - B + 1)
    between = np.take_along_axis(ends + np.arange(B - 1), rng.integers(0, B - 1, (N, 8, E, 1)), axis=3)[:, :, :, 0]
    e = rng.permutation(N)
    long = np.arange(E)
    long = long[long % 4 < 2]
    for r in range(N):
        h = rng.permutation(8)
        a[r, h[0]] = 1
        a[r, h[1]] = E
        a[r, h[2]] = 1
        a[r, h[2], ::2, 0] = E - 1
        a[r, h[2], 1::2, B - 1] = E - 1
        a[r, h[2], long] = E
        a[r, h[2], long, long % 2 * (B - 1)] = E - 1
        gap[r, h[2], long] = (long // 4 + rng.integers(2)) % 2 * (E - 1)
        a[r, h[3]] = E // 2
        a[r, h[4]] = rng.integers(1, E + 1, (E, B))
        a[r, h[5]] = full[r, h[5]]
        gap[r, h[5], ::2] = between[r, h[5], ::2]
        a[r, h[6]] = E // B
    a[e[0]] = E
    a[e[1]] = full[e[1]]
    gap[e[1]] = between[e[1]]
    z = rng.integers(0, 2, (N, 8, E, E))
    np.put_along_axis(z, gap[:, :, :, None], -1, axis=3)
    x[:, :, 0, :, 0] = z.reshape(N, 8, C).astype(np.float32).astype(BF)
    u[:, :, ::16] = 0
    for h in range(0, 128, 16): u[:, h, h, 0] = 1
    return {"x": x.reshape(N, 128, 4 * C), "u": u.reshape(N, 128, 512), "v": d["v"], **weights(rng, [0]), **blocks(a)}
def setup_inputs_spread(rng):
    d = setup_inputs(rng)
    d["x"] = wide(rng, N, 128, 4 * C, cols=6)
    return d
def check_inputs(d):
    b = []
    for k in ("x", "u", "v"):
        a = np.abs(d[k].astype(np.float32))
        if not (np.isfinite(a).all() and ((a == 0) | (a >= 2.0 ** -30) & (a <= 2.0 ** 30)).all()): b.append("a value of " + k)
    if ((d["wc"] & 0x7F) == 0x7F).any(): b.append("a code of wc that is no number")
    none, least, most = [emit(mx_ref.quantize(np.full((128, 16), k, np.float32).astype(BF)))[1][0, 0] for k in (0.0, 2.0 ** -30, 2.0 ** 30)]
    for r in range(N):
        s = mx_ref.live(d["ws"][r])
        if ((s != none) & ((s < least) | (s > most))).any(): b.append("a scale of ws")
    if ((d["bl"] < 1) | (d["bl"] > E)).any(): b.append("a length in bl")
    return b
def reference(x, u, v, wc, ws, bl):
    qu = [mx_ref.quantize(u[r]) for r in range(N)]
    lay = [pk(wc[r], ws[r]) for r in range(N)]
    size = [gentries(bl[r]).reshape(8, E, B).astype(int) for r in range(N)]
    now = [x[r] for r in range(N)]
    for t in range(R):
        own, sent, bound = [], [], []
        for r in range(N):
            q = mx_ref.quantize(now[r])
            a = decode(q).astype(BF)
            e, h, first, last = solve(size[r], gaps(mx_ref.matmul(qu[r], q)))
            z = ((gcols(a, e).astype(np.float32) + gcols(a, h).astype(np.float32)) * np.float32(0.5)).astype(BF)
            own.append(a)
            sent.append(mx_ref.quantize(z))
            bound.append((first, last))
        for r in range(N):
            p = r ^ STEP[t]
            e = fallen(bound[p][0], bound[p][1])
            made = []
            for b in range(4):
                h = mx_ref.matmul(pick(lay[r], np.arange(128 * b, 128 * b + 128)), sent[p]) * np.float32(0.03125)
                h = np.concatenate([h, np.zeros((128, 1), np.float32)], axis=1)
                made.append(own[r][:, b::4].astype(np.float32) + gpick(h, e))
            now[r] = tile(made)
    y, ob = np.zeros((N, 128, C), np.float32), np.zeros((N, 8, 2 * K), np.float32)
    oc, osc = np.zeros((N, 128, 4 * C), np.uint8), np.zeros((N, 16, C), np.uint8)
    for r in range(N):
        q = mx_ref.quantize(now[r])
        y[r] = mx_ref.matmul(mx_ref.quantize(v[r]), q)
        ob[r] = np.stack([bound[r][0], bound[r][1]], axis=3).reshape(8, 2 * K)
        oc[r], osc[r] = emit(q)
    return {"y": y, "ob": ob, "oc": oc, "osc": osc}

from concourse.bass import DstId, RemoteDMATransfer
from concourse.mybir import dt, AluOpType, ActivationFunctionType

A = AluOpType
COPY = ActivationFunctionType.Copy
IDENT = ActivationFunctionType.Identity
RELU = ActivationFunctionType.Relu
C, E, K, R = 400, 20, 80, 3
STEP = [1, 2, 4]
HALF = 240
PART = ((0, HALF), (HALF, C))
TP, HP = 416, 96
ZW = 4 * K
XA, LA = 128, 128 + C
F32, BF, I32, U16, MXC, U8 = "float32", "bfloat16", "int32", "uint16", "float8_e4m3fn_x4", "uint8"

SCRATCH = {}


def _buf(name, n, dtype, where="sbuf"):
    SCRATCH[name] = (where, [128, n], dtype)


for _t in range(R + 1):
    _buf("X%d" % _t, 4 * C, BF)
    _buf("QX%d" % _t, LA + K, MXC)
    _buf("SX%d" % _t, LA + ZW, U8)
for _t in range(R):
    _buf("M%d" % _t, 64, BF)
    _buf("LM%d" % _t, 64, BF)
    _buf("LN%d" % _t, 32, BF)
for _n, _w, _d in [
    ("RC", K, MXC), ("RS", ZW, U8), ("RM", 32, BF), ("RN", 16, BF), ("SN", 32, BF), ("B", 64, F32), ("BO", 64, F32),
    ("UT", 512, BF), ("QU", 128, MXC), ("SU", 128, U8), ("QP", 128, MXC), ("SP", 128, U8),
    ("VT", 512, BF), ("QV", 128, MXC), ("SV", 128, U8), ("QW", 512, MXC), ("SW", 512, U8),
    ("E0", 520, BF), ("E1", 520, BF), ("ONES", 128, BF), ("QE", 512, MXC), ("SE", 512, U8),
    ("Z", 512, BF), ("TH", 4 * TP, BF), ("TF", 2 * C, BF), ("MH", 4 * K, F32),
    ("HS", 4 * HP, F32), ("GS", 2 * C, F32), ("YS", C, F32),
    ("P", 408, F32), ("NR", C, BF), ("W3", 496, BF), ("RS1", C, F32), ("DEC", C, BF),
    ("PI", 8, I32), ("IC", 8, I32), ("FC", 40, F32), ("IO", 512, F32), ("TM", 896, F32), ("LF", 64, F32),
    ("OFS", 64, U16), ("OZ", 16, U16), ("GL", 32, U16), ("BLI", 8, I32), ("BLU", 8, U16), ("NW", 32, F32),
    ("UN", K, F32), ("N1", K, F32), ("N2", K, F32), ("N3", 136, F32), ("NA", 64, F32),
    ("XS", K, F32), ("XD", 64, F32), ("XM", 24, F32), ("KC", 576, F32),
    ("EG", 64, F32), ("EX", 72, F32), ("TD0", 128, BF), ("TD1", 128, BF), ("TO", 128, BF),
    ("D0", 384, F32), ("D1", 384, F32), ("O", 384, F32), ("FN", 640, F32),
    ("J", 208, F32), ("WW", 200, BF), ("KP", 200, BF), ("CC", 208, BF), ("CW", 200, BF), ("CS", 200, BF),
    ("OW", 32, F32), ("OBI", 16, U16), ("OBU", 256, F32), ("OBF", 160, F32),
]:
    _buf(_n, _w, _d)
_buf("PT", 2048, F32, "psum")
_buf("PH", 2048, F32, "psum")

POOL = {"v": 48, "s": 36, "t": 14, "g": 22}
NDMA = 17
SEMAPHORES = [e + str(i) for e in "vstg" for i in range(POOL[e])] + ["d%d" % i for i in range(NDMA)] \
    + [n + str(t) for n in ("az", "al", "an") for t in range(R)] + ["rz", "rl", "rn", "sent"]


def bits(engines):
    m = 0
    for e in engines:
        m |= 1 << e
    return m


def relays(core, far, topo):
    if topo.may_write(core, far):
        return []
    return [c for c in topo.cores_of(core) if c != core and topo.die(c) == topo.die(core) and topo.may_write(c, far)]


def to(topo, dst, src):
    rid, pid = topo.addr(dst, src)
    return DstId(rid=rid, pnc=pid)


def relay_program(g, core, T, topo):
    for r, c in enumerate(T.cores):
        for t in range(R):
            far = T.cores[r ^ STEP[t]]
            via = relays(c, far, topo)
            if core not in via[:2]:
                continue
            rid, pid = topo.addr(far, core)
            m, n = topo.mask(core, far), len(topo.engines(core, far))
            inn, h = len(topo.engines(c, core)) // 2, via.index(core)
            g.wait_ge(T.sem.rn, inn)
            g.remote_dma(T["LN%d" % t][:, 16 * h:16 * h + 16], T.RN[:], T.sem["an%d" % t], T.sem.sent, pid, rid, m)
            g.wait_ge(T.sem.rl, inn)
            g.remote_dma(T["LM%d" % t][:, 32 * h:32 * h + 32], T.RM[:], T.sem["al%d" % t], T.sem.sent, pid, rid, m)
            g.wait_ge(T.sem.rz, inn)
            if h == 0:
                g.remote_dma(T["QX%d" % t][:, LA:LA + K].bitcast(dt.uint8), T.RC[:].bitcast(dt.uint8), T.sem["az%d" % t], T.sem.sent, pid, rid, m)
            else:
                g.remote_dma(T["SX%d" % t][:, LA:LA + K], T.RS[:, 0:K], T.sem["az%d" % t], T.sem.sent, pid, rid, m)
            g.wait_ge(T.sem.sent, 3 * n)


def rank_program(g, core, T, topo):
    rank = T.rank_of(core)
    if rank is None:
        relay_program(g, core, T, topo)
        return
    queue = {"v": g.vector, "s": g.scalar, "t": g.tensor, "g": g, "y": g.sync}
    ops, last, readers, touched = [], {}, {}, {}

    def V(name, a=0, b=None, st=1):
        b = SCRATCH[name][1][1] if b is None else b
        ap = T[name][:, a:b:st] if st > 1 else T[name][:, a:b]
        return (ap, name, range(a, b, st))

    def words(v):
        return (v[0].bitcast(dt.uint32), v[1], v[2])

    def ind(win, off):
        return (win[0].indirect(off[0]), win[1], win[2], off)

    def op(eng, fn, rd=(), wr=(), ext=(), dma=False):
        n, deps = len(ops), set()
        rd = [v for v in rd if isinstance(v, tuple)]
        rd = rd + [v[3] for v in rd if len(v) > 3]
        for v in rd + list(wr):
            if SCRATCH[v[1]][0] == "psum":
                for bank in set(c // 512 for c in v[2]):
                    seen = touched.setdefault((v[1], bank), [])
                    deps.update(o for o in seen if ops[o]["eng"] != eng)
                    seen.append(n)
        for v in rd:
            for c in v[2]:
                if (v[1], c) in last:
                    deps.add(last[(v[1], c)])
        for v in wr:
            for c in v[2]:
                if (v[1], c) in last:
                    deps.add(last[(v[1], c)])
                deps.update(readers.pop((v[1], c), ()))
        for v in rd:
            for c in v[2]:
                readers.setdefault((v[1], c), []).append(n)
        for v in wr:
            for c in v[2]:
                last[(v[1], c)] = n
        deps.discard(n)
        ops.append({"eng": eng, "fn": fn, "deps": deps, "ext": list(ext), "dma": dma, "signal": False})
        return n

    def ap(v):
        return v[0] if isinstance(v, tuple) else v

    def ts(out, in0, s1, op0, s2=None, op1=None, ext=()):
        if op1 is None:
            return op("v", lambda: g.vector.tensor_scalar(out[0], in0[0], ap(s1), None, op0), [in0, s1], [out], ext)
        return op("v", lambda: g.vector.tensor_scalar(out[0], in0[0], ap(s1), ap(s2), op0, op1), [in0, s1, s2], [out], ext)

    def tt(out, in0, in1, o, ext=()):
        return op("v", lambda: g.vector.tensor_tensor(out[0], in0[0], in1[0], o), [in0, in1], [out], ext)

    def cp(out, in_):
        return op("v", lambda: g.vector.tensor_copy(out[0], in_[0]), [in_], [out])

    def ms(out, x):
        return op("v", lambda: g.vector.memset(out[0], x), [], [out])

    def scan(out, d0, d1, init, op0, op1):
        return op("v", lambda: g.vector.tensor_tensor_scan(out[0], d0[0], d1[0], init, op0, op1), [d0, d1], [out])

    def act(out, in_, func=COPY, bias=None, scale=None):
        kw = {}
        if bias is not None:
            kw["bias"] = ap(bias)
        if scale is not None:
            kw["scale"] = ap(scale)
        return op("s", lambda: g.scalar.activation(out[0], in_[0], func, **kw), [in_, bias, scale], [out])

    def aff(out, in_, scale, bias):
        return act(out, in_, IDENT, bias, scale)

    def fill(out, x):
        return aff(out, V("ONES", 0, len(out[2])), 0.0, x)

    def iota(out, pattern, base=0, cm=0):
        if SCRATCH[out[1]][2] == I32:
            return op("g", lambda: g.iota(out[0], pattern, base, cm), [], [out])
        return op("g", lambda: g.iota(out[0], pattern, base, cm, allow_small_or_imprecise_dtypes=True), [], [out])

    def quant(q, s, x):
        return op("v", lambda: g.vector.quantize_mx(q[0], s[0], x[0]), [x], [q, s])

    def mm(out, wq, wsc, xq, xsc, ext=()):
        return op("t", lambda: g.tensor.matmul_mx(out[0], wq[0], wsc[0], xq[0], xsc[0], True, True), [wq, wsc, xq, xsc], [out], ext)

    def load(eng, out, src, codes=False, after=()):
        dst = out[0].bitcast(dt.uint8) if codes else out[0]
        return op(eng, lambda: queue[eng].dma_start(dst, src), after, [out], dma=True)

    stores = []

    def store(eng, dst, src, rd):
        stores.append(op(eng, lambda: queue[eng].dma_start(dst, src), [rd], [], dma=True))

    load("y", V("X0", 0, 4 * HALF), T.x[:, 0:4 * HALF])
    load("s", V("UT"), T.u[:])
    load("s", V("BLI", 0, 5), T.bl[:])
    load("y", V("X0", 4 * HALF, 4 * C), T.x[:, 4 * HALF:4 * C])
    load("y", V("QW"), T.wc[:], codes=True, after=[V("X0")])
    load("y", V("SW"), T.ws[:])
    load("y", V("VT"), T.v[:])

    IOA, IO4 = V("IO", 0, 80), V("IO", 80, 160)
    iota(V("PI", 0, 1), [[0, 1]], 0, 1)
    iota(IO4, [[0, 20], [1, 4]])
    iota(IOA, [[1, 80]])
    ms(V("ONES"), 1.0)
    ms(V("E0"), 0.0)
    eye = V("E0", 2, 514, 4)
    op("g", lambda: g.affine_select(eye[0], T.ONES[:], [[-1, 128]], A.is_equal, 0.0, 0, 1), [V("ONES")], [eye])
    iota(V("IO", 160, 192), [[0, 4], [1, 8]])
    iota(V("LF", 0, 8), [[16, 8]])
    iota(V("NW"), [[4096, 32]])
    fill(V("P", 0, 1), -1e25)
    fill(V("N3", 85, 136), 1.0)
    fill(V("W3", 401, 496), 64.0)
    fill(V("EX", 64, 72), 0.0)
    fill(V("E1", 0, 1), 0.0)
    fill(V("TD0", 0, 128, 2), 0.0)
    fill(V("KC", 193, 384, 3), 0.0)
    fill(V("KC", 194, 384, 3), -128.0)
    p = V("PI", 0, 1)
    ts(V("IC", 0, 1), p, 3, A.bitwise_and)
    ts(V("IC", 1, 2), p, 2, A.logical_shift_right, 3, A.bitwise_and)
    ts(V("IC", 2, 3), p, 3, A.logical_shift_right, 1, A.bitwise_and)
    ts(V("IC", 3, 4), p, 1, A.bitwise_and)
    ts(V("IC", 4, 5), p, 15, A.bitwise_and)
    ts(V("IC", 5, 6), p, 1, A.logical_shift_right, 3, A.bitwise_and)
    cp(V("FC", 0, 6), V("IC", 0, 6))
    m_, s_, hb, q1, q_, k2 = [V("FC", i, i + 1) for i in range(6)]
    col = [V("FC", i, i + 1) for i in range(6, 40)]
    OU, L1, L2, L3, L5, L7 = [V("OFS", a, b) for a, b in ((0, 8), (8, 12), (12, 16), (16, 18), (18, 23), (24, 28))]
    L4, L6 = V("OFS", 28, 41), V("OFS", 42, 52)
    m20, m19, m40, mb = col[0:4]
    ts(m20, m_, 20.0, A.mult)
    ts(m19, m_, 20.0, A.mult, 19.0, A.add)
    aff(m40, m_, 1280.0, 1280.0)
    aff(mb, m_, -40960.0, 2048.0)
    aff(col[4], hb, 1.0, m_)
    act(V("TM", 360, 440), IOA, RELU, m40, -64.0)
    act(V("TM", 440, 520), IOA, RELU, mb, 2048.0)
    aff(V("TM", 524, 530), V("IO", 0, 6), 1.0, m_)
    aff(V("TM", 520, 524), V("IO", 0, 8, 2), 1.0, col[4])
    aff(V("TM", 530, 562), V("IO", 160, 192), 1.0, s_)
    act(V("E1", 1, 520), V("E0", 0, 519))
    ts(V("TM", 0, 80), IO4, s_, A.is_equal, 1023.0, A.mult)
    ts(V("TM", 80, 160), IO4, s_, A.is_ge)
    ts(V("TM", 160, 180), V("IO", 80, 100), m_, A.is_equal, 1023.0, A.mult)
    ts(V("TM", 180, 200), V("IO", 80, 100), m_, A.is_ge)
    ts(V("TM", 200, 280), IOA, m20, A.is_equal, 1e29, A.mult)
    ts(V("TM", 280, 360), IOA, m19, A.is_equal, -1e25, A.mult)
    tt(V("XS"), V("TM", 0, 80), V("TM", 80, 160), A.add)
    tt(V("XM", 0, 20), V("TM", 160, 180), V("TM", 180, 200), A.add)
    tt(V("RS1", 0, 80), V("TM", 200, 280), V("TM", 280, 360), A.add)
    ts(V("TM", 562, 604), V("TM", 520, 562), 5.0, A.is_ge, -5.0, A.mult)
    cp(OU, V("LF", 0, 8))
    tt(V("TM", 604, 646), V("TM", 520, 562), V("TM", 562, 604), A.add)
    tt(V("DEC", 0, 80), V("TM", 360, 440), V("TM", 440, 520), A.min)
    ts(V("KC", 560, 564), V("IO", 80, 84), s_, A.not_equal, -9999.0, A.mult)
    ts(V("XM", 3, 20, 4), V("XM", 3, 20, 4), 2.0 ** -16, A.mult)
    aff(col[5], s_, 20.0, 3.0)
    aff(col[6], q1, -8.0, 4.0)
    aff(col[7], q_, 8.0, 0.0)
    aff(col[8], q_, 12.0, 296.0)
    aff(col[9], q_, 4.0, 0.0)
    aff(col[10], q1, 4.0, col[7])
    aff(col[11], hb, -192.0, col[8])
    fill(V("LF", 12, 16), col[9])
    aff(V("LF", 18, 24), V("TM", 608, 614), 4.0, col[5])
    aff(V("LF", 8, 12), V("TM", 604, 608), 80.0, 0.0)
    aff(V("LF", 24, 28), V("IO", 0, 4), col[6], col[10])
    aff(V("LF", 16, 18), V("IO", 0, 2), -192.0, col[11])

    def unit(b):
        quant(V("QE", 128 * b, 128 * b + 128), V("SE", 128 * b, 128 * b + 128), V("E%d" % (b % 2), 2 - 2 * (b // 2), 514 - 2 * (b // 2)))

    unit(0)
    unit(2)
    cp(V("BLU", 0, 5), V("BLI", 0, 5))
    quant(V("QU"), V("SU"), V("UT"))
    act(V("UN"), ind(V("NW"), V("BLU", 0, 5)))
    act(V("SP"), ind(V("SU"), OU))
    cp(words(V("QP")), ind(words(V("QU")), OU))
    for a in range(1, 5):
        act(V("RS1", 80 * a, 80 * a + 80), V("RS1", 0, 80))
    aff(V("XS", 3, 80, 4), V("XS", 3, 80, 4), 2.0 ** -16, 0.0)
    cc = col[14:]
    aff(cc[0], q_, 0.05, -0.475)
    aff(cc[1], s_, 0.2, -0.4)
    aff(cc[2], hb, -1.0, 0.0)
    aff(cc[4], s_, 16.0, m_)
    aff(cc[5], k2, 16.0, q1)

    def quant_x(t, h):
        a, b = PART[h]
        quant(V("QX%d" % t, XA + a, XA + b), V("SX%d" % t, XA + a, XA + b), V("X%d" % t, 4 * a, 4 * b))

    def scores(t, wq, wsc):
        for h, (a, b) in enumerate(PART):
            mm(V("PH", 512 * h, 512 * h + b - a), wq, wsc, V("QX%d" % t, XA + a, XA + b), V("SX%d" % t, XA + a, XA + b))

    NA, NK = V("NA"), V("NA", 0, 64, 2)
    K1, K2, K3 = V("KC", 0, 64), V("KC", 64, 128), V("KC", 128, 192)
    A1, A2, T2, T2S, AD = [V("KC", 384 + 32 * i, 416 + 32 * i) for i in range(5)]

    def tables_a():
        cp(V("OFS", 8, 28), V("LF", 8, 28))
        for k in range(4):
            scan(V("N1", 20 * k, 20 * k + 20), V("UN", k, 80, 4), V("XM", 0, 20), 0.0, A.max, A.mult)
        act(V("N2"), ind(V("N1"), L5))
        for a in range(1, 5):
            act(V("DEC", 80 * a, 80 * a + 80), V("DEC", 0, 80))
        act(V("XD"), V("XS", 0, 64))
        aff(V("XD", 3, 64, 8), V("XS", 3, 64, 8), -1.0, 0.0)

    def tables_b():
        scan(V("N3", 5, 85), V("N2"), V("XS"), 0.0, A.max, A.mult)
        act(NA, ind(V("N3", 8, 136), L7))
        aff(V("SN"), NK, 1.0, -1.0)
        for d, cb in ((0, 20.0), (1, -1.0)):
            aff(V("KC", 128 + d, 192, 2), V("NA", d, 64, 2), -1.0, 19.0 - cb)
            aff(V("KC", d, 64, 2), V("NA", d, 64, 2), -1.0, 32.0 + cb)
        aff(V("TD1", 0, 128, 2), NA, -1.0, 52.0)
        for d, cb in ((0, 20.0), (1, -1.0)):
            aff(V("KC", 64 + d, 128, 2), V("NA", d, 64, 2), 1.0, 34.0 + cb)
        aff(V("D1", 1, 96, 6), V("NA", 0, 16), 1.0, 33.0)
        fill(V("D1", 3, 96, 6), 32.0)
        fill(V("D0", 0, 384, 6), 0.0)
        aff(V("KC", 192, 384, 3), NA, 1.0, 1.0)
        aff(col[12], m_, 20.0, -17.0)
        aff(col[13], m_, 20.0, 15.0)
        aff(A2, NK, 1.0, 53.0)
        act(T2, NK, ActivationFunctionType.Square, -1.0)
        aff(V("TM", 646, 678), V("TM", 614, 646), 80.0, col[12])
        aff(AD, V("TM", 614, 646), 80.0, col[13])
        for k in range(4):
            aff(V("KC", 480 + 8 * k, 488 + 8 * k), V("KC", 448 + 8 * k, 456 + 8 * k), 1.0, V("KC", 560 + k, 561 + k))

    def patterns():
        iota(V("D1"), [[0, 384]])
        iota(V("D0"), [[0, 384]], 1)
        iota(V("IO", 200, 240), [[16, 5], [0, 8]])
        iota(V("IO", 240, 280), [[-1, 5], [-1, 4], [0, 2]], 10)
        iota(V("IO", 280, 293), [[-2, 13]], 30)
        for k in range(4):
            iota(V("O", 96 * k + 60, 96 * k + 96), [[0, 36]])
        iota(V("IO", 328, 368), [[0, 20], [-1, 2]], 1)
        iota(V("IO", 368, 408), [[-16, 5], [-12, 4], [0, 2]], 168)
        iota(V("IO", 464, 472), [[4, 4], [2, 2]])
        iota(V("IO", 472, 474), [[2, 2]], 44)
        for b in range(4):
            iota(V("TH", TP * b, TP * b + 16), [[0, 16]])
        iota(V("Z", 4 * K, 512), [[0, 192]])

    def patterns_late():
        iota(V("KP"), [[0, 200]], 1)
        iota(V("J", 200, 208), [[0, 8]])
        iota(V("LF", 41, 42), [[0, 1]])
        for b in range(4):
            iota(V("HS", HP * b, HP * b + 8), [[0, 8]])

    def tables_c():
        aff(V("IO", 408, 421), V("IO", 280, 293), 1.0, cc[2])
        aff(V("TM", 0, 40), V("IO", 200, 240), 0.05, cc[0])
        aff(V("TM", 40, 80), V("IO", 240, 280), 0.2, cc[1])
        aff(V("TM", 80, 93), V("IO", 408, 421), 0.2, -0.4)
        aff(cc[6], k2, 64.0, hb)
        aff(V("TM", 100, 193), V("TM", 0, 93), 1.0, 12582912.0)
        aff(cc[7], q1, 16.0, cc[6])
        aff(V("TM", 200, 293), V("TM", 100, 193), 1.0, -12582912.0)
        aff(V("LF", 42, 52), V("IO", 464, 474), 1.0, cc[7])
        act(V("TM", 300, 340), V("TM", 200, 240))
        aff(V("TM", 340, 380), V("TM", 240, 280), -80.0, cc[4])
        aff(V("TM", 380, 393), V("TM", 280, 293), -5.0, 0.0)

    def tables_d():
        aff(V("LF", 28, 41), V("TM", 480, 493), 2.0, cc[5])
        for a in range(5):
            aff(V("J", 40 * a, 40 * a + 40), V("TM", 400, 440), 1.0, 4.0 * a)
        act(V("WW", 0, 40, 2), V("TM", 440, 480, 2))
        aff(V("WW", 1, 40, 2), V("TM", 441, 480, 2), -1.0, 0.0)
        fill(V("KP", 0, 200, 8), 0.0)
        for a in range(1, 5):
            act(V("WW", 40 * a, 40 * a + 40), V("WW", 0, 40))

    sent = [0]

    def send(t, src, land, hop, n, sem, hsem):
        far = T.cores[rank ^ STEP[t]]
        via = relays(core, far, topo)
        if via:
            en = topo.engines(core, via[0])
            k = len(en) // 2
            tr = [RemoteDMATransfer(dst_ids=[to(topo, via[h], core)], dma_engine_mask=bits(en[k * h:k * h + k]), remote_sem=T.sem[hsem],
                                    src=T[src][:, n // 2 * h:n // 2 * (h + 1)], dst=T[hop][:]) for h in range(2)]
            op("g", lambda: g.remote_dma_fused(tr, local_sem=T.sem.sent), [V(src)])
        else:
            en = topo.engines(core, far)
            rid, pid = topo.addr(far, core)
            op("g", lambda: g.remote_dma(T[land][:], T[src][:], T.sem[sem], T.sem.sent, pid, rid, bits(en)), [V(src)])
        sent[0] += len(en)

    def cover(first, msg, nm1, ext, ext2):
        rn, mx, fl = [V("FN", 160 + 32 * i, 192 + 32 * i) for i in range(3)]
        ts(rn, V(msg, 1, 64, 2), -1.0, A.mult, ext=ext)
        tt(mx, V(msg, 0, 64, 2), rn, A.max)
        tt(fl, V(msg, 0, 64, 2), rn, A.min)
        tt(first, mx, nm1, A.subtract, ext2)
        return fl

    patterns()
    quant_x(0, 0)
    quant_x(0, 1)
    for t in range(R):
        far = T.cores[rank ^ STEP[t]]
        via = relays(core, far, topo)
        q, sc, M = "QX%d" % t, "SX%d" % t, "M%d" % t
        scores(t, V("QP"), V("SP"))
        if t == 0:
            tables_a()
        for h, (a, b) in enumerate(PART):
            scan(V("P", a + 1, b + 1), V("RS1", a, b), V("PH", 512 * h, 512 * h + b - a), -1e25, A.add, A.min)
        if t == 0:
            tables_b()
        for h, (a, b) in enumerate(PART):
            tt(V("NR", a, b), V("PH", 512 * h, 512 * h + b - a), V("P", a, b), A.is_ge)
        for a, b in PART:
            scan(V("W3", a + 1, b + 1), V("NR", a, b), V("DEC", a, b), 0.0, A.mult, A.max)
        if t == 0:
            tables_c()
            for u in range(R):
                send(u, "SN", "LN%d" % u, "RN", 32, "an%d" % u, "rn")
            patterns_late()
            unit(1)
            unit(3)
        for b in range(4):
            mm(V("PT", 512 * b, 512 * b + C), V("QE", 128 * b, 128 * b + 128), V("SE", 128 * b, 128 * b + 128), V(q, XA, LA), V(sc, XA, LA))
        for b in range(4):
            aff(V("TH", TP * b + 16, TP * b + TP), V("PT", 512 * b, 512 * b + C), 0.5, 0.0)
        cp(V("EG"), ind(V("W3", 80, 496), L1))
        scan(V("EX", 5, 69), V("EG"), V("XD"), 0.0, A.max, A.mult)
        w = ind(V("EX", 8, 72), L2)
        tt(V("TD0", 1, 128, 2), w, K3, A.is_le)
        tt(V("TD1", 1, 128, 2), w, K1, A.add)
        tt(V("D1", 0, 384, 6), w, K2, A.add)
        scan(V("TO"), V("TD0"), V("TD1"), 0.0, A.mult, A.max)
        for k in range(4):
            a = 96 * k
            t1, t2 = V("TD1", 32 * k + 1, 32 * k + 20, 2), V("TO", 32 * k + 1, 32 * k + 20, 2)
            hit, fit = V("D0", a + 1, a + 60, 6), V("D0", a + 2, a + 60, 6)
            if k == 0:
                ts(hit, t1, 32.0, A.is_lt)
                ts(fit, t2, 32.0, A.is_ge)
            else:
                f = V("O", a - 93, a - 36, 6)
                tt(hit, f, t1, A.is_gt)
                tt(fit, f, t2, A.is_le)
                tt(V("D1", a + 1, a + 60, 2), V("O", a - 93, a - 34, 2), V("KC", 192 + 48 * k, 222 + 48 * k), A.add)
            scan(V("O", a, a + 60), V("D0", a, a + 60), V("D1", a, a + 60), 0.0, A.mult, A.max)
            if t == 0 and k == 2:
                tt(A1, V("TM", 646, 678), NK, A.subtract)
        DF, LM, RN, SQ, SS = [V("FN", 32 * i, 32 * i + 32) for i in range(5)]
        FB, MR, peL = V(M, 0, 64, 2), V(M, 1, 64, 2), V("O", 2, 384, 12)
        tt(MR, ind(V("O"), L3), A2, A.subtract)
        ts(FB, peL, -33.0, A.add)
        send(t, M, "LM%d" % t, "RM", 64, "al%d" % t, "rl")
        tt(LM, peL, A1, A.add)
        tt(DF, FB, MR, A.add)
        tt(RN, AD, MR, A.subtract)
        tt(SQ, DF, DF, A.mult)
        tt(SS, SQ, T2S, A.is_le)
        tt(V("FN", 416, 480, 2), SS, LM, A.mult)
        tt(V("FN", 417, 480, 2), SS, RN, A.mult)
        tt(V("FN", 480, 512), V("FN", 416, 448), V("FN", 448, 480), A.add)
        tt(V("FN", 512, 528), V("FN", 480, 496), V("FN", 496, 512), A.add)
        OM, ON = V("OZ", 0, 5), V("OZ", 6, 11)
        cp(OM, V("FN", 512, 522, 2))
        cp(ON, V("FN", 513, 522, 2))
        if t == 0:
            tt(V("TM", 400, 493), V("TM", 300, 393), V("IO", 328, 421), A.add)
        if t == 1:
            quant(V("QV"), V("SV"), V("VT"))
        if via:
            en = topo.engines(core, via[0])
            ends = [(via[0], T.RC[:], T.sem.rz), (via[1], T.RS[:], T.sem.rz)]
        else:
            en = topo.engines(core, far)
            ends = [(far, T[q][:, LA:LA + K], T.sem["az%d" % t]), (far, T[sc][:, LA:LA + ZW], T.sem["az%d" % t])]
        nz = sum(len(topo.engines(c, core)) for c in (relays(far, core, topo)[:2] or [far]))
        for b in range(4):
            act(V("MH", K * b, K * b + K), ind(V("TH", TP * b, TP * b + TP), OM))
        for b in range(4):
            tt(V("Z", b, 4 * K, 4), ind(V("TH", TP * b, TP * b + TP), ON), V("MH", K * b, K * b + K), A.add)
        quant(V(q, 0, 128), V(sc, 0, 128), V("Z"))
        zc, zs = V(q, 0, K), V(sc, 0, ZW)
        tr = [RemoteDMATransfer(dst_ids=[to(topo, ends[0][0], core)], dma_engine_mask=bits(en[:len(en) // 2]), remote_sem=ends[0][2],
                                src=zc[0].bitcast(dt.uint8), dst=ends[0][1].bitcast(dt.uint8)),
              RemoteDMATransfer(dst_ids=[to(topo, ends[1][0], core)], dma_engine_mask=bits(en[len(en) // 2:]), remote_sem=ends[1][2],
                                src=zs[0], dst=ends[1][1])]
        op("g", lambda tr=tr: g.remote_dma_fused(tr, local_sem=T.sem.sent), [zc, zs])
        sent[0] += len(en)
        if t == 0:
            tables_d()
            cp(V("OFS", 28, 52), V("LF", 28, 52))
        for b in range(2):
            act(V("TF", C * b, C * b + C), V("PT", 512 * b, 512 * b + C))
        if t == 1:
            iota(V("OW"), [[1, 32]], -1)
        fl = cover(V("B", 0, 64, 2), "LM%d" % t, V("LN%d" % t), [("al%d" % t, nz)], [("an%d" % t, nz)])
        ts(SQ, V("B", 0, 64, 2), -1.0, A.add)
        tt(V("B", 1, 64, 2), fl, SQ, A.max)
        tt(V("CC"), ind(V("B"), L4), V("J"), A.is_le)
        tt(V("CW"), V("CC", 0, 200), V("WW"), A.mult)
        scan(V("CS"), V("KP"), V("CW"), 0.0, A.mult, A.add)
        ll = V("GL", 0, 25)
        cp(ll, V("CS", 7, 200, 8))
        if t == R - 1:
            fl = cover(DF, M, V("SN"), [], [])
            tt(SS, DF, fl, A.is_le)
            tt(V("BO", 0, 64, 2), DF, SS, A.mult)
            tt(V("BO", 1, 64, 2), fl, SS, A.mult)
            for k in range(4):
                cp(V("OBI", 4 * k, 4 * k + 4), V("BO", 16 * k, 16 * k + 4))
        lc, ls = V(q, LA + K - 128, LA + K), V(sc, LA + K - 128, LA + K)
        for i, b in enumerate((0, 2, 1, 3)):
            mm(V("PH", 512 * b, 512 * b + 128), V("QW", 128 * b, 128 * b + 128), V("SW", 128 * b, 128 * b + 128), lc, ls,
               [("az%d" % t, nz)] if i == 0 else [])
        X = "X%d" % (t + 1)
        ts(V("HS", 8, 88), V("PH", 48, 128), 0.03125, A.mult)
        for b in (2, 1, 3):
            aff(V("HS", HP * b + 8, HP * b + 88), V("PH", 512 * b + 48, 512 * b + 128), 0.03125, 0.0)
        for b in range(2, 4):
            act(V("GS", C * (b - 2), C * (b - 1)), ind(V("HS", HP * b, HP * b + 88), ll))
        if t == R - 1:
            act(V("OBU"), ind(V("OW"), V("OBI")))
            act(V("OBF"), ind(V("OBU"), L6))
        for b in range(2):
            tt(V(X, b, 4 * C, 4), ind(V("HS", HP * b, HP * b + 88), ll), V("TF", C * b, C * b + C), A.add)
        for b, a, e in ((2, 0, C), (3, 0, HALF), (3, HALF, C)):
            tt(V(X, 4 * a + b, 4 * e, 4), V("PT", 512 * b + a, 512 * b + e), V("GS", C * (b - 2) + a, C * (b - 2) + e), A.add)
        quant_x(t + 1, 0)
        quant_x(t + 1, 1)

    scores(R, V("QV"), V("SV"))
    q, sc = "QX%d" % R, "SX%d" % R
    store("y", T.ob[:], T.OBF[0:128:16, :], V("OBF"))
    for a, b in PART:
        store("y", T.oc[:, 4 * a:4 * b], T[q][:, XA + a:XA + b].bitcast(dt.uint8), V(q, XA + a, XA + b))
    for k in range(4):
        store("y", T.osc[4 * k:4 * k + 4, :], T[sc][32 * k:32 * k + 4, XA:LA], V(sc, XA, LA))
    act(V("YS", 0, HALF), V("PH", 0, HALF))
    store("s", T.y[:, 0:HALF], T.YS[:, 0:HALF], V("YS", 0, HALF))
    cp(V("YS", HALF, C), V("PH", 512, 512 + C - HALF))
    store("s", T.y[:, HALF:C], T.YS[:, HALF:C], V("YS", HALF, C))

    known = {e: set() for e in queue}
    for n, o in enumerate(ops):
        kn, need = known[o["eng"]], []
        for d in sorted(o["deps"], reverse=True):
            if d not in kn:
                need.append(d)
                ops[d]["signal"] = True
                kn.add(d)
                kn.update(ops[d]["known"])
        o["need"], o["known"] = need, set(kn)
    for n in stores:
        ops[n]["signal"] = True
    count, holder, turn, nd = {}, {}, {e: 0 for e in POOL}, [0]
    for n, o in enumerate(ops):
        e, qu = o["eng"], queue[o["eng"]]
        for d in o["need"]:
            qu.wait_ge(T.sem[ops[d]["sem"]], ops[d]["val"])
        for name, val in o["ext"]:
            qu.wait_ge(T.sem[name], val)
        if not o["signal"]:
            o["fn"]()
            continue
        if o["dma"]:
            name, inc = "d%d" % nd[0], 16
            nd[0] += 1
        else:
            names = [e + str((turn[e] + i) % POOL[e]) for i in range(POOL[e])]
            free = [x for x in names if x not in holder or holder[x] in o["known"]]
            if not free:
                free = names
                qu.wait_ge(T.sem[names[0]], count[names[0]])
            name, inc = free[0], 1
            turn[e] = (int(name[1:]) + 1) % POOL[e]
            holder[name] = n
        count[name] = count.get(name, 0) + inc
        o["sem"], o["val"] = name, count[name]
        o["fn"]().then_inc(T.sem[name], inc)
    for n in stores:
        g.sync.wait_ge(T.sem[ops[n]["sem"]], ops[n]["val"])
    g.wait_ge(T.sem.sent, sent[0])
